import numpy as np
import ml_dtypes

BF16 = ml_dtypes.bfloat16


def bf(x):
    return np.asarray(x, np.float32).astype(BF16)


def f32(x):
    return np.asarray(x, np.float32)


def f64(x):
    return np.asarray(x).astype(np.float64)


def striped(idx):
    return np.concatenate([l.reshape(-1, 16).T for l in idx])


def rows(idx, k):
    return np.tile(np.repeat(idx, 16, axis=0), (k // (16 * 8), 1))


def look(tab, idx):
    return np.take_along_axis(f64(tab), rows(idx, len(tab)), axis=1)


P, K, S, V, N = 128, 128, 2048, 1024, 1024


def setup_inputs():
    return {"tab": f32(0.5 * np.random.standard_normal((K, S))), "u": f32(0.3 * np.random.standard_normal((K, V))), "e": bf(np.tile(np.eye(16), (8, 1))), "offs": striped(np.random.randint(0, S, (8, N)))}


def reference(tab, u, e, offs):
    idx = np.stack([g.T.reshape(-1) for g in np.split(offs, 8)])
    s = look(tab, idx) + f64(u)
    s = np.concatenate([f64(e).T @ s[a:a + P] for a in range(0, K, P)])
    x = np.exp(-s)
    return x

@@ -1,0 +1,36 @@
+import concourse.mybir as mybir
+
+F32, BF16, U16 = mybir.dt.float32, mybir.dt.bfloat16, mybir.dt.uint16
+PIECE = 512
+GROUP = 16
+FLOPS = 2 * 128 * 16 * 1024
+
+
+def tile_lookup_adc_exp_out_kernel(tc, tab, u, e, offs, out):
+    nc = tc.nc
+    rows, codewords = tab.shape
+    queries, vectors = out.shape
+    with (
+        tc.tile_pool(name="held", bufs=1) as held,
+        tc.psum_pool(name="psum", bufs=1) as psum,
+    ):
+        offsets = held.tile([rows, vectors // GROUP], U16, name="offsets")
+        table = held.tile([rows, codewords], F32, name="table")
+        correction = held.tile([rows, vectors], F32, name="correction")
+        member16 = held.tile([rows, queries], BF16, name="member16")
+        member = held.tile([rows, queries], F32, name="member")
+        nc.sync.dma_start(offsets[:], offs)
+        nc.sync.dma_start(table[:], tab)
+        nc.sync.dma_start(correction[:], u)
+        nc.scalar.dma_start(member16[:], e)
+        nc.vector.tensor_copy(member[:], member16[:])
+        weights = held.tile([queries, vectors], F32, name="weights")
+        for piece in range(vectors // PIECE):
+            cols = slice(piece * PIECE, (piece + 1) * PIECE)
+            picked = table[:].indirect(offsets[:, cols.start // GROUP : cols.stop // GROUP])
+            sums = held.tile([rows, PIECE], F32, name=f"sums{piece}")
+            nc.vector.tensor_tensor(sums[:], picked, correction[:, cols], mybir.AluOpType.add)
+            score = psum.tile([queries, PIECE], F32, name=f"score{piece}")
+            nc.tensor.matmul(score[:], member[:], sums[:], start=True, stop=True)
+            nc.scalar.activation(weights[:, cols], score[:], mybir.ActivationFunctionType.Exp, scale=-1.0)
+        nc.sync.dma_start(out, weights[:])

@@ -3,6 +3,7 @@ import concourse.mybir as mybir
 F32, BF16, U16 = mybir.dt.float32, mybir.dt.bfloat16, mybir.dt.uint16
 PIECE = 512
 GROUP = 16
+QUADRANT = 32
 FLOPS = 2 * 128 * 16 * 1024
 
 
@@ -10,27 +11,42 @@ def tile_lookup_adc_exp_out_kernel(tc, tab, u, e, offs, out):
     nc = tc.nc
     rows, codewords = tab.shape
     queries, vectors = out.shape
+    pieces = vectors // PIECE
+    quadrants = rows // QUADRANT
+    width = PIECE // quadrants
     with (
         tc.tile_pool(name="held", bufs=1) as held,
         tc.psum_pool(name="psum", bufs=1) as psum,
     ):
         offsets = held.tile([rows, vectors // GROUP], U16, name="offsets")
         table = held.tile([rows, codewords], F32, name="table")
-        correction = held.tile([rows, vectors], F32, name="correction")
-        member16 = held.tile([rows, queries], BF16, name="member16")
-        member = held.tile([rows, queries], F32, name="member")
+        member = held.tile([rows, queries], BF16, name="member")
         nc.sync.dma_start(offsets[:], offs)
         nc.sync.dma_start(table[:], tab)
-        nc.sync.dma_start(correction[:], u)
-        nc.scalar.dma_start(member16[:], e)
-        nc.vector.tensor_copy(member[:], member16[:])
-        weights = held.tile([queries, vectors], F32, name="weights")
-        for piece in range(vectors // PIECE):
-            cols = slice(piece * PIECE, (piece + 1) * PIECE)
-            picked = table[:].indirect(offsets[:, cols.start // GROUP : cols.stop // GROUP])
+        corrections = []
+        for piece in range(pieces):
+            correction = held.tile([rows, PIECE], F32, name=f"correction{piece}")
+            nc.sync.dma_start(correction[:], u[:, piece * PIECE : (piece + 1) * PIECE])
+            corrections.append(correction)
+        nc.scalar.dma_start(member[:], e)
+
+        spread = held.tile([rows, QUADRANT + pieces], F32, name="spread")
+        nc.vector.memset(spread[:], 0.0)
+        nc.vector.tensor_copy(spread[:, pieces - 1 : QUADRANT + pieces - 1 : pieces], member[:])
+
+        score = psum.tile([rows, width], F32, name="score")
+        for piece in range(pieces):
+            picked = table[:].indirect(offsets[:, piece * PIECE // GROUP : (piece + 1) * PIECE // GROUP])
             sums = held.tile([rows, PIECE], F32, name=f"sums{piece}")
-            nc.vector.tensor_tensor(sums[:], picked, correction[:, cols], mybir.AluOpType.add)
-            score = psum.tile([queries, PIECE], F32, name=f"score{piece}")
-            nc.tensor.matmul(score[:], member[:], sums[:], start=True, stop=True)
-            nc.scalar.activation(weights[:, cols], score[:], mybir.ActivationFunctionType.Exp, scale=-1.0)
-        nc.sync.dma_start(out, weights[:])
+            nc.vector.tensor_tensor(sums[:], picked, corrections[piece][:], mybir.AluOpType.add)
+            for quadrant in range(quadrants):
+                nc.tensor.matmul(
+                    score[quadrant * QUADRANT : (quadrant + 1) * QUADRANT, :],
+                    spread[:, pieces - 1 - piece : pieces - 1 - piece + QUADRANT],
+                    sums[:, quadrant * width : (quadrant + 1) * width],
+                    start=piece == 0,
+                    stop=piece == pieces - 1,
+                )
+        weights = held.tile([rows, width], F32, name="weights")
+        nc.scalar.activation(weights[:], score[:], mybir.ActivationFunctionType.Exp, scale=-1.0)
+        nc.sync.dma_start(out.rearrange("t (h q j) -> q (t h) j", h=pieces, q=quadrants), weights[:])

@@ -12,8 +12,9 @@ def tile_lookup_adc_exp_out_kernel(tc, tab, u, e, offs, out):
     rows, codewords = tab.shape
     queries, vectors = out.shape
     pieces = vectors // PIECE
-    quadrants = rows // QUADRANT
-    width = PIECE // quadrants
+    chunks = rows // queries
+    width = PIECE // chunks
+    shared = QUADRANT // queries
     with (
         tc.tile_pool(name="held", bufs=1) as held,
         tc.psum_pool(name="psum", bufs=1) as psum,
@@ -30,23 +31,29 @@ def tile_lookup_adc_exp_out_kernel(tc, tab, u, e, offs, out):
             corrections.append(correction)
         nc.scalar.dma_start(member[:], e)
 
-        spread = held.tile([rows, QUADRANT + pieces], F32, name="spread")
+        spread = held.tile([rows, 3 * queries], F32, name="spread")
         nc.vector.memset(spread[:], 0.0)
-        nc.vector.tensor_copy(spread[:, pieces - 1 : QUADRANT + pieces - 1 : pieces], member[:])
+        nc.vector.tensor_copy(spread[:, queries : 2 * queries], member[:])
 
-        score = psum.tile([rows, width], F32, name="score")
+        warm = psum.tile([rows, PIECE], F32, name="warm")
+        nc.tensor.matmul(warm[:], table[:, :rows], table[:, :PIECE], start=True, stop=True)
+
+        placed = out.rearrange("t (h c j) -> h c t j", h=pieces, c=chunks)
         for piece in range(pieces):
             picked = table[:].indirect(offsets[:, piece * PIECE // GROUP : (piece + 1) * PIECE // GROUP])
             sums = held.tile([rows, PIECE], F32, name=f"sums{piece}")
             nc.vector.tensor_tensor(sums[:], picked, corrections[piece][:], mybir.AluOpType.add)
-            for quadrant in range(quadrants):
-                nc.tensor.matmul(
-                    score[quadrant * QUADRANT : (quadrant + 1) * QUADRANT, :],
-                    spread[:, pieces - 1 - piece : pieces - 1 - piece + QUADRANT],
-                    sums[:, quadrant * width : (quadrant + 1) * width],
-                    start=piece == 0,
-                    stop=piece == pieces - 1,
-                )
-        weights = held.tile([rows, width], F32, name="weights")
-        nc.scalar.activation(weights[:], score[:], mybir.ActivationFunctionType.Exp, scale=-1.0)
-        nc.sync.dma_start(out.rearrange("t (h q j) -> q (t h) j", h=pieces, q=quadrants), weights[:])
+            score = psum.tile([rows, width], F32, name=f"score{piece}")
+            for half in range(shared):
+                for quadrant in range(rows // QUADRANT):
+                    chunk = quadrant * shared + half
+                    nc.tensor.matmul(
+                        score[quadrant * QUADRANT : (quadrant + 1) * QUADRANT, :],
+                        spread[:, (1 - half) * queries : (1 - half) * queries + QUADRANT],
+                        sums[:, chunk * width : (chunk + 1) * width],
+                        start=half == 0,
+                        stop=half == shared - 1,
+                    )
+            weights = held.tile([rows, width], F32, name=f"weights{piece}")
+            nc.scalar.activation(weights[:], score[:], mybir.ActivationFunctionType.Exp, scale=-1.0)
+            nc.sync.dma_start(placed[piece], weights[:])

@@ -22,8 +22,8 @@ def tile_lookup_adc_exp_out_kernel(tc, tab, u, e, offs, out):
         offsets = held.tile([rows, vectors // GROUP], U16, name="offsets")
         table = held.tile([rows, codewords], F32, name="table")
         member = held.tile([rows, queries], BF16, name="member")
-        nc.sync.dma_start(offsets[:], offs)
         nc.sync.dma_start(table[:], tab)
+        nc.sync.dma_start(offsets[:], offs)
         corrections = []
         for piece in range(pieces):
             correction = held.tile([rows, PIECE], F32, name=f"correction{piece}")
@@ -56,4 +56,4 @@ def tile_lookup_adc_exp_out_kernel(tc, tab, u, e, offs, out):
                     )
             weights = held.tile([rows, width], F32, name=f"weights{piece}")
             nc.scalar.activation(weights[:], score[:], mybir.ActivationFunctionType.Exp, scale=-1.0)
-            nc.sync.dma_start(placed[piece], weights[:])
+            nc.scalar.dma_start(placed[piece], weights[:])

import concourse.mybir as mybir

F32, BF16, U16 = mybir.dt.float32, mybir.dt.bfloat16, mybir.dt.uint16
PIECE = 512
GROUP = 16
QUADRANT = 32
FLOPS = 2 * 128 * 16 * 1024


def tile_lookup_adc_exp_out_kernel(tc, tab, u, e, offs, out):
    nc = tc.nc
    rows, codewords = tab.shape
    queries, vectors = out.shape
    pieces = vectors // PIECE
    chunks = rows // queries
    width = PIECE // chunks
    shared = QUADRANT // queries
    with (
        tc.tile_pool(name="held", bufs=1) as held,
        tc.psum_pool(name="psum", bufs=1) as psum,
    ):
        offsets = held.tile([rows, vectors // GROUP], U16, name="offsets")
        table = held.tile([rows, codewords], F32, name="table")
        member = held.tile([rows, queries], BF16, name="member")
        nc.sync.dma_start(table[:], tab)
        nc.sync.dma_start(offsets[:], offs)
        corrections = []
        for piece in range(pieces):
            correction = held.tile([rows, PIECE], F32, name=f"correction{piece}")
            nc.sync.dma_start(correction[:], u[:, piece * PIECE : (piece + 1) * PIECE])
            corrections.append(correction)
        nc.scalar.dma_start(member[:], e)

        spread = held.tile([rows, 3 * queries], F32, name="spread")
        nc.vector.memset(spread[:], 0.0)
        nc.vector.tensor_copy(spread[:, queries : 2 * queries], member[:])

        warm = psum.tile([rows, PIECE], F32, name="warm")
        nc.tensor.matmul(warm[:], table[:, :rows], table[:, :PIECE], start=True, stop=True)

        placed = out.rearrange("t (h c j) -> h c t j", h=pieces, c=chunks)
        for piece in range(pieces):
            picked = table[:].indirect(offsets[:, piece * PIECE // GROUP : (piece + 1) * PIECE // GROUP])
            sums = held.tile([rows, PIECE], F32, name=f"sums{piece}")
            nc.vector.tensor_tensor(sums[:], picked, corrections[piece][:], mybir.AluOpType.add)
            score = psum.tile([rows, width], F32, name=f"score{piece}")
            for half in range(shared):
                for quadrant in range(rows // QUADRANT):
                    chunk = quadrant * shared + half
                    nc.tensor.matmul(
                        score[quadrant * QUADRANT : (quadrant + 1) * QUADRANT, :],
                        spread[:, (1 - half) * queries : (1 - half) * queries + QUADRANT],
                        sums[:, chunk * width : (chunk + 1) * width],
                        start=half == 0,
                        stop=half == shared - 1,
                    )
            weights = held.tile([rows, width], F32, name=f"weights{piece}")
            nc.scalar.activation(weights[:], score[:], mybir.ActivationFunctionType.Exp, scale=-1.0)
            nc.scalar.dma_start(placed[piece], weights[:])
